import numpy as np
import ml_dtypes


def mxq(x, axis, fmt="e4m3"):
    dtype, down = {"e4m3": (ml_dtypes.float8_e4m3fn, 7), "e5m2": (ml_dtypes.float8_e5m2, 14)}[fmt]
    v = np.moveaxis(np.asarray(x, np.float32).astype(ml_dtypes.bfloat16).astype(np.float64), axis, -1)
    blocks = v.reshape(v.shape[:-1] + (-1, 32))
    amax = np.abs(blocks).max(-1, keepdims=True)
    byte = np.maximum(np.where(amax > 0, np.frexp(amax)[1] - 1 + 127, 0) - down, 1)
    scale = np.exp2(byte - 127.0)
    codes = (blocks / scale).astype(np.float32).astype(dtype).astype(np.float64)
    return np.moveaxis((codes * scale).reshape(v.shape), -1, axis)


WIDE = False


def mx_kscale(k, group=512):
    if not WIDE:
        return np.ones(k)
    levels = np.array([18, -18])
    if group != 512:
        return np.exp2(np.random.permutation(np.resize(levels, k // group))).repeat(group)
    if k % 512:
        return np.exp2(np.random.permutation(np.resize(levels, k // 32))).repeat(32)
    a = np.empty((k // 512, 16))
    for p in range(k // 512):
        a[p, :8] = np.random.permutation(np.resize(levels, 8))
        for g in range(8):
            far = levels[np.abs(levels - a[p, g]) >= 10]
            a[p, g + 8] = far[np.random.randint(len(far))]
    return np.exp2(a.ravel()).repeat(32)


def f64(x):
    return np.asarray(x).astype(np.float64)


def bf(x):
    return np.asarray(x, np.float32).astype(ml_dtypes.bfloat16)


def planes(Y):
    r, m = Y.shape
    b = f64(bf(Y)).reshape(r // 32, 32, m)
    amax = np.abs(b).max(1)
    byte = np.clip(np.where(amax > 0, np.frexp(amax)[1] - 1 + 127 - 7, 1), 1, 254)
    codes = (b * np.exp2(127.0 - byte)[:, None, :]).reshape(r, m).astype(np.float32).astype(ml_dtypes.float8_e4m3fn).view(np.uint8)
    words = codes.reshape(r // 512, 128, 4, m).transpose(0, 1, 3, 2)
    return np.ascontiguousarray(words), np.ascontiguousarray(byte.astype(np.uint8).reshape(r // 512, 16, m))


G, D, I, N, J = 4, 128, 128, 512, 128


def sgn(shape):
    return np.random.uniform(0.5, 2.0, shape) * np.where(np.random.standard_normal(shape) < 0, -1.0, 1.0)


def setup_inputs():
    n = np.random.standard_normal
    s_d = mx_kscale(D, 0)
    s_i = mx_kscale(I, 0)
    return {
        "x": (n((G, D, I)) * s_d[:, None]).astype(np.float32),
        "w": (n((D, N)) / np.sqrt(D) / s_d[:, None]).astype(np.float32),
        "ni": (sgn((G, I, 1)) * s_i[:, None]).astype(np.float32),
        "ad": ((np.random.uniform(size=(G, I, J)) < 0.1) * np.random.uniform(0.5, 1.0, (G, I, J)) / 3 / s_i[:, None]).astype(np.float32),
        "wo": (n((D, N)) / np.sqrt(D) / s_d[:, None]).astype(np.float32),
        "nj": (np.random.uniform(0.5, 2.0, (G, J, 1))).astype(np.float32),
    }


def reference(x, w, ni, ad, wo, nj):
    xq = mxq(f64(x), 1, "e4m3")
    wq = mxq(f64(w), 0, "e4m3")
    z = xq.transpose(0, 2, 1) @ wq
    h = z * f64(ni)
    adq = mxq(f64(ad), 1, "e4m3")
    hq = mxq(h, 1, "e4m3")
    y = adq.transpose(0, 2, 1) @ hq
    woq = mxq(f64(wo), 0, "e4m3")
    o = xq.transpose(0, 2, 1) @ woq
    out_ = np.maximum(y * f64(nj) + o, 0.0)
    Y = out_.reshape(G * J, N)
    words, scales = planes(Y)
    return Y, words, scales

@@ -1,0 +1,223 @@
+from contextlib import ExitStack
+
+import concourse.mybir as mybir
+
+G, D, NODES, N = 4, 128, 128, 512
+FLOPS = 3 * 2 * G * D * NODES * N
+
+F32 = mybir.dt.float32
+BF16 = mybir.dt.bfloat16
+I32 = mybir.dt.int32
+U32 = mybir.dt.uint32
+U8 = mybir.dt.uint8
+FP8X4 = mybir.dt.float8_e4m3fn_x4
+ACT = mybir.ActivationFunctionType
+ALU = mybir.AluOpType
+
+P = 128
+PACK = 4
+ROWS = 32
+HALF = N // 2
+MM_N = 128
+SCALE_WORDS = HALF // 4
+VECTOR_COLS = 176
+
+
+def rows_of(g):
+    return slice(ROWS * g, ROWS * (g + 1))
+
+
+def interleave_views(dst, src, lo, hi):
+    out = dst[:, PACK * lo : PACK * hi].rearrange("p (c i t) -> p c t i", i=4, t=PACK)
+    in_ = src[:, :, lo:hi].rearrange("p t (c i) -> p c t i", i=4)
+    return out, in_
+
+
+def interleave_shared(nc, dst, src):
+    out, in_ = interleave_views(dst, src, 0, VECTOR_COLS)
+    nc.vector.tensor_copy(out=out, in_=in_)
+    out, in_ = interleave_views(dst, src, VECTOR_COLS, HALF)
+    nc.scalar.copy(out=out, in_=in_)
+
+
+def tile_rows_pl_gnn_sage_kernel(tc, x, w, ni, ad, wo, nj, out_0, out_1, out_2):
+    nc = tc.nc
+    with ExitStack() as ctx:
+        sb = ctx.enter_context(tc.tile_pool(name="sb", bufs=1))
+        ps = ctx.enter_context(tc.psum_pool(name="ps", bufs=1))
+        ctx.enter_context(tc.manual_schedule())
+
+        def tile(name, shape, dtype):
+            return sb.tile(shape, dtype, name=name, align_bytes=64)
+
+        bank_a = [ps.tile([P, N], F32, name="bank_a%d" % g) for g in range(G)]
+        bank_b = [ps.tile([P, N], F32, name="bank_b%d" % g) for g in range(G)]
+
+        w_raw = tile("w_raw", [P, PACK, HALF], F32)
+        x_raw = tile("x_raw", [P, PACK, NODES], F32)
+        ad_raw = tile("ad_raw", [P, PACK, NODES], F32)
+        ni_col = tile("ni_col", [P, G], F32)
+        nj_col = tile("nj_col", [P, G], F32)
+        for h in range(2):
+            cols = slice(HALF * h, HALF * (h + 1))
+            nc.sync.dma_start(out=w_raw[rows_of(h), :, :], in_=w[:, cols].rearrange("(p j) n -> p j n", j=PACK))
+            nc.scalar.dma_start(out=w_raw[rows_of(2 + h), :, :], in_=wo[:, cols].rearrange("(p j) n -> p j n", j=PACK))
+        nc.sync.dma_start(out=x_raw[:], in_=x.rearrange("g (p j) i -> (g p) j i", j=PACK))
+        nc.sync.dma_start(out=ad_raw[:], in_=ad.rearrange("g (p j) i -> (g p) j i", j=PACK))
+        with nc.allow_non_contiguous_dma(reason="one factor a node, nodes on the partitions"):
+            nc.scalar.dma_start(out=ni_col[:], in_=ni.rearrange("g i o -> i (g o)"))
+            nc.scalar.dma_start(out=nj_col[:], in_=nj.rearrange("g i o -> i (g o)"))
+
+        home = tile("home", [P, HALF + SCALE_WORDS], U32)
+        across = tile("across", [P, HALF + SCALE_WORDS], U32)
+        near = [tile("near%d" % k, [P, HALF + SCALE_WORDS], U32) for k in range(2)]
+        nc.vector.memset(home[:, HALF:], 0)
+        w_bf = tile("w_bf", [P, PACK * HALF], BF16)
+        interleave_shared(nc, w_bf, w_raw)
+        nc.vector.quantize_mx(out=home[:, :HALF].bitcast(FP8X4), scales=home[:, HALF:].bitcast(U8), in_=w_bf[:])
+
+        def move(engine, dst, dst_row, src_row, count):
+            engine.dma_start(
+                out=dst[dst_row : dst_row + count, :].bitcast(I32),
+                in_=home[src_row : src_row + count, :].bitcast(I32),
+            )
+
+        def spread(k, first, second):
+            base = 64 * k
+            move(first, near[k], 32, base, 64)
+            move(second, across, 64 - base, base, 64)
+            move(first, near[k], 96, base, 32)
+            move(second, near[k], 0, base + 32, 32)
+
+        spread(0, nc.sync, nc.scalar)
+        spread(1, nc.sync, nc.sync)
+
+        def weight_piece(k, h, g):
+            quadrant = 2 * k + h
+            if g == quadrant:
+                return home
+            if g == (quadrant + 2) % G:
+                return across
+            return near[k]
+
+        x_bf = tile("x_bf", [P, PACK * NODES], BF16)
+        ad_bf = tile("ad_bf", [P, PACK * NODES], BF16)
+        x_codes = tile("x_codes", [P, NODES], U32)
+        x_scales = tile("x_scales", [P, NODES], U8)
+        ad_codes = tile("ad_codes", [P, NODES], U32)
+        ad_scales = tile("ad_scales", [P, NODES], U8)
+        for dst, src in ((x_bf, x_raw), (ad_bf, ad_raw)):
+            out, in_ = interleave_views(dst, src, 0, NODES)
+            nc.vector.tensor_copy(out=out, in_=in_)
+        nc.vector.quantize_mx(out=x_codes[:].bitcast(FP8X4), scales=x_scales[:], in_=x_bf[:])
+        nc.vector.quantize_mx(out=ad_codes[:].bitcast(FP8X4), scales=ad_scales[:], in_=ad_bf[:])
+
+        def product(g, out, lhs_codes, lhs_scales, rhs_codes, rhs_scales):
+            r = rows_of(g)
+            nc.tensor.matmul_mx(
+                out=out,
+                lhsT=lhs_codes[r, :].bitcast(FP8X4),
+                lhsT_scale=lhs_scales[r, :],
+                rhs=rhs_codes[r, :].bitcast(FP8X4),
+                rhs_scale=rhs_scales[r, :],
+                start=True,
+                stop=True,
+            )
+
+        def features_times_weights(k, banks):
+            for c in range(N // MM_N):
+                h, first = divmod(c * MM_N, HALF)
+                for g in range(G):
+                    piece = weight_piece(k, h, g)
+                    product(
+                        g,
+                        banks[g][:, c * MM_N : (c + 1) * MM_N],
+                        x_codes,
+                        x_scales,
+                        piece[:, first : first + MM_N],
+                        piece[:, HALF:].bitcast(U8)[:, first : first + MM_N],
+                    )
+
+        features_times_weights(0, bank_a)
+        features_times_weights(1, bank_b)
+
+        h_rows = [tile("h_rows%d" % h, [P, PACK, HALF], BF16) for h in range(2)]
+        for h in range(2):
+            cols = slice(HALF * h, HALF * (h + 1))
+            for g in (0, 2, 1, 3):
+                h_nodes = tile("h_nodes%d_%d" % (g, h), [P, HALF], BF16)
+                if g < 2:
+                    nc.scalar.activation(out=h_nodes[:], in_=bank_a[g][:, cols], func=ACT.Copy, scale=ni_col[:, g : g + 1])
+                else:
+                    nc.vector.tensor_scalar(
+                        out=h_nodes[:], in0=bank_a[g][:, cols], scalar1=ni_col[:, g : g + 1], scalar2=None, op0=ALU.mult
+                    )
+                nc.sync.dma_start(out=h_rows[h][rows_of(g), :, :], in_=h_nodes[:])
+
+        own = [tile("own%d" % g, [P, N], F32) for g in range(G)]
+        for g in (0, 2, 1, 3):
+            if g < 2:
+                nc.scalar.copy(out=own[g][:], in_=bank_b[g][:])
+            else:
+                nc.vector.tensor_copy(out=own[g][:], in_=bank_b[g][:])
+
+        h_codes = tile("h_codes", [P, N], U32)
+        h_scales = tile("h_scales", [P, N], U8)
+        y_banks = (bank_a, bank_b)
+        for h in range(2):
+            cols = slice(HALF * h, HALF * (h + 1))
+            h_bf = tile("h_bf%d" % h, [P, PACK * HALF], BF16)
+            interleave_shared(nc, h_bf, h_rows[h])
+            nc.vector.quantize_mx(out=h_codes[:, cols].bitcast(FP8X4), scales=h_scales[:, cols], in_=h_bf[:])
+            for c in range(HALF // MM_N):
+                first = HALF * h + c * MM_N
+                for g in range(G):
+                    product(
+                        g,
+                        y_banks[h][g][:, c * MM_N : (c + 1) * MM_N],
+                        ad_codes,
+                        ad_scales,
+                        h_codes[:, first : first + MM_N],
+                        h_scales[:, first : first + MM_N],
+                    )
+
+        pre = [tile("pre%d" % g, [P, N], F32) for g in range(G)]
+        res_rows = [tile("res_rows%d" % h, [P, PACK, HALF], BF16) for h in range(2)]
+        for h in range(2):
+            cols = slice(HALF * h, HALF * (h + 1))
+            for g in range(G):
+                nc.vector.scalar_tensor_tensor(
+                    out=pre[g][:, cols],
+                    in0=y_banks[h][g][:, :HALF],
+                    scalar=nj_col[:, g : g + 1],
+                    in1=own[g][:, cols],
+                    op0=ALU.mult,
+                    op1=ALU.add,
+                )
+                res_nodes = tile("res_nodes%d_%d" % (g, h), [P, HALF], BF16)
+                nc.scalar.activation(out=res_nodes[:], in_=pre[g][:, cols], func=ACT.Relu)
+                nc.sync.dma_start(out=res_rows[h][rows_of(g), :, :], in_=res_nodes[:])
+
+        for g in range(G):
+            res = tile("res%d" % g, [P, N], F32)
+            if g < 3:
+                nc.vector.tensor_scalar_max(out=res[:], in0=pre[g][:], scalar1=0.0)
+            else:
+                nc.scalar.activation(out=res[:], in_=pre[g][:], func=ACT.Relu)
+            nc.sync.dma_start(out=out_0[NODES * g : NODES * (g + 1), :], in_=res[:])
+
+        words = out_1[0].rearrange("p n u -> p (n u)").bitcast(I32)
+        scale_rows = out_2[0].bitcast(I32)
+        res_codes = tile("res_codes", [P, N], U32)
+        res_scales = tile("res_scales", [P, N], U8)
+        for h in range(2):
+            cols = slice(HALF * h, HALF * (h + 1))
+            res_bf = tile("res_bf%d" % h, [P, PACK * HALF], BF16)
+            interleave_shared(nc, res_bf, res_rows[h])
+            nc.vector.quantize_mx(out=res_codes[:, cols].bitcast(FP8X4), scales=res_scales[:, cols], in_=res_bf[:])
+            nc.sync.dma_start(out=words[:, cols], in_=res_codes[:, cols].bitcast(I32))
+        for q in range(G):
+            engine = nc.scalar if q < 2 else nc.sync
+            engine.dma_start(
+                out=scale_rows[4 * q : 4 * q + 4, :], in_=res_scales[ROWS * q : ROWS * q + 4, :].bitcast(I32)
+            )

@@ -33,11 +33,16 @@ def interleave_views(dst, src, lo, hi):
     return out, in_
 
 
-def interleave_shared(nc, dst, src):
-    out, in_ = interleave_views(dst, src, 0, VECTOR_COLS)
-    nc.vector.tensor_copy(out=out, in_=in_)
-    out, in_ = interleave_views(dst, src, VECTOR_COLS, HALF)
+def interleave_shared(nc, dst, src, vector_cols=VECTOR_COLS):
+    if vector_cols:
+        out, in_ = interleave_views(dst, src, 0, vector_cols)
+        nc.vector.tensor_copy(out=out, in_=in_)
+    out, in_ = interleave_views(dst, src, vector_cols, HALF)
     nc.scalar.copy(out=out, in_=in_)
+
+
+def half_cols(h):
+    return slice(HALF * h, HALF * (h + 1))
 
 
 def tile_rows_pl_gnn_sage_kernel(tc, x, w, ni, ad, wo, nj, out_0, out_1, out_2):
@@ -50,31 +55,38 @@ def tile_rows_pl_gnn_sage_kernel(tc, x, w, ni, ad, wo, nj, out_0, out_1, out_2):
         def tile(name, shape, dtype):
             return sb.tile(shape, dtype, name=name, align_bytes=64)
 
-        bank_a = [ps.tile([P, N], F32, name="bank_a%d" % g) for g in range(G)]
-        bank_b = [ps.tile([P, N], F32, name="bank_b%d" % g) for g in range(G)]
+        banks = [[ps.tile([P, N], F32, name="bank%d_%d" % (ph, g)) for g in range(G)] for ph in range(2)]
+        first, second = slice(0, HALF), slice(HALF, N)
 
         w_raw = tile("w_raw", [P, PACK, HALF], F32)
         x_raw = tile("x_raw", [P, PACK, NODES], F32)
         ad_raw = tile("ad_raw", [P, PACK, NODES], F32)
-        ni_col = tile("ni_col", [P, G], F32)
-        nj_col = tile("nj_col", [P, G], F32)
-        for h in range(2):
-            cols = slice(HALF * h, HALF * (h + 1))
-            nc.sync.dma_start(out=w_raw[rows_of(h), :, :], in_=w[:, cols].rearrange("(p j) n -> p j n", j=PACK))
-            nc.scalar.dma_start(out=w_raw[rows_of(2 + h), :, :], in_=wo[:, cols].rearrange("(p j) n -> p j n", j=PACK))
-        nc.sync.dma_start(out=x_raw[:], in_=x.rearrange("g (p j) i -> (g p) j i", j=PACK))
-        nc.sync.dma_start(out=ad_raw[:], in_=ad.rearrange("g (p j) i -> (g p) j i", j=PACK))
-        with nc.allow_non_contiguous_dma(reason="one factor a node, nodes on the partitions"):
-            nc.scalar.dma_start(out=ni_col[:], in_=ni.rearrange("g i o -> i (g o)"))
-            nc.scalar.dma_start(out=nj_col[:], in_=nj.rearrange("g i o -> i (g o)"))
-
+        factor_rows = tile("factor_rows", [P, ROWS], F32)
+        factors = tile("factors", [P, ROWS], F32)
         home = tile("home", [P, HALF + SCALE_WORDS], U32)
         across = tile("across", [P, HALF + SCALE_WORDS], U32)
         near = [tile("near%d" % k, [P, HALF + SCALE_WORDS], U32) for k in range(2)]
+        nc.vector.memset(factor_rows[:], 0.0)
         nc.vector.memset(home[:, HALF:], 0)
-        w_bf = tile("w_bf", [P, PACK * HALF], BF16)
-        interleave_shared(nc, w_bf, w_raw)
-        nc.vector.quantize_mx(out=home[:, :HALF].bitcast(FP8X4), scales=home[:, HALF:].bitcast(U8), in_=w_bf[:])
+
+        def load_factor(src, row):
+            nc.scalar.dma_start(out=factor_rows[row:P:8, :], in_=src.rearrange("g (q b) o -> q g (b o)", b=ROWS))
+
+        for h in range(2):
+            nc.sync.dma_start(out=w_raw[rows_of(h), :, :], in_=w[:, half_cols(h)].rearrange("(p j) n -> p j n", j=PACK))
+            nc.scalar.dma_start(out=w_raw[rows_of(2 + h), :, :], in_=wo[:, half_cols(h)].rearrange("(p j) n -> p j n", j=PACK))
+        nc.sync.dma_start(out=x_raw[:], in_=x.rearrange("g (p j) i -> (g p) j i", j=PACK))
+        nc.sync.dma_start(out=ad_raw[:], in_=ad.rearrange("g (p j) i -> (g p) j i", j=PACK))
+        load_factor(ni, 0)
+        load_factor(nj, 4)
+        warm = tile("warm", [P, 1], F32)
+        nc.scalar.activation(out=warm[:], in_=home[:, HALF : HALF + 1], func=ACT.Relu)
+
+        def ni_of(g):
+            return factors[:, 8 * g : 8 * g + 1]
+
+        def nj_of(g):
+            return factors[:, 8 * g + 4 : 8 * g + 5]
 
         def move(engine, dst, dst_row, src_row, count):
             engine.dma_start(
@@ -82,15 +94,12 @@ def tile_rows_pl_gnn_sage_kernel(tc, x, w, ni, ad, wo, nj, out_0, out_1, out_2):
                 in_=home[src_row : src_row + count, :].bitcast(I32),
             )
 
-        def spread(k, first, second):
+        def spread(k, one, other):
             base = 64 * k
-            move(first, near[k], 32, base, 64)
-            move(second, across, 64 - base, base, 64)
-            move(first, near[k], 96, base, 32)
-            move(second, near[k], 0, base + 32, 32)
-
-        spread(0, nc.sync, nc.scalar)
-        spread(1, nc.sync, nc.sync)
+            move(one, near[k], 32, base, 64)
+            move(other, across, 64 - base, base, 64)
+            move(other, near[k], 96, base, 32)
+            move(one, near[k], 0, base + 32, 32)
 
         def weight_piece(k, h, g):
             quadrant = 2 * k + h
@@ -100,124 +109,139 @@ def tile_rows_pl_gnn_sage_kernel(tc, x, w, ni, ad, wo, nj, out_0, out_1, out_2):
                 return across
             return near[k]
 
+        def products(lhs, rhs_of, ph, cols, graphs):
+            lhs_codes, lhs_scales = lhs
+            for c in range(0, HALF, MM_N):
+                for g in graphs:
+                    r = rows_of(g)
+                    rhs_codes, rhs_scales = rhs_of(g)
+                    nc.tensor.matmul_mx(
+                        out=banks[ph][g][:, cols.start + c : cols.start + c + MM_N],
+                        lhsT=lhs_codes[r, :].bitcast(FP8X4),
+                        lhsT_scale=lhs_scales[r, :],
+                        rhs=rhs_codes[r, c : c + MM_N].bitcast(FP8X4),
+                        rhs_scale=rhs_scales[r, c : c + MM_N],
+                        start=True,
+                        stop=True,
+                    )
+
+        def weight_products(k, h, graphs):
+            def rhs_of(g):
+                piece = weight_piece(k, h, g)
+                return piece[:, :HALF], piece[:, HALF:].bitcast(U8)
+
+            products(x_mx, rhs_of, h, (first, second)[k], graphs)
+
+        def edge_products(h, graphs):
+            products(ad_mx, lambda g: (h_codes[h], h_scales[h]), h, first, graphs)
+
+        w_bf = tile("w_bf", [P, PACK * HALF], BF16)
         x_bf = tile("x_bf", [P, PACK * NODES], BF16)
         ad_bf = tile("ad_bf", [P, PACK * NODES], BF16)
-        x_codes = tile("x_codes", [P, NODES], U32)
-        x_scales = tile("x_scales", [P, NODES], U8)
-        ad_codes = tile("ad_codes", [P, NODES], U32)
-        ad_scales = tile("ad_scales", [P, NODES], U8)
-        for dst, src in ((x_bf, x_raw), (ad_bf, ad_raw)):
-            out, in_ = interleave_views(dst, src, 0, NODES)
-            nc.vector.tensor_copy(out=out, in_=in_)
-        nc.vector.quantize_mx(out=x_codes[:].bitcast(FP8X4), scales=x_scales[:], in_=x_bf[:])
-        nc.vector.quantize_mx(out=ad_codes[:].bitcast(FP8X4), scales=ad_scales[:], in_=ad_bf[:])
+        x_mx = (tile("x_codes", [P, NODES], U32), tile("x_scales", [P, NODES], U8))
+        ad_mx = (tile("ad_codes", [P, NODES], U32), tile("ad_scales", [P, NODES], U8))
+        h_rows = [tile("h_rows%d" % ph, [P, PACK, HALF], BF16) for ph in range(2)]
+        h_bf = [tile("h_bf%d" % ph, [P, PACK * HALF], BF16) for ph in range(2)]
+        h_codes = [tile("h_codes%d" % ph, [P, HALF], U32) for ph in range(2)]
+        h_scales = [tile("h_scales%d" % ph, [P, HALF], U8) for ph in range(2)]
+        own = [tile("own%d" % g, [P, N], F32) for g in range(G)]
+        pre = [tile("pre%d" % g, [P, N], F32) for g in range(G)]
+        res = [tile("res%d" % k, [P, 2, N], F32) for k in range(2)]
+        res_rows = [tile("res_rows%d" % ph, [P, PACK, HALF], BF16) for ph in range(2)]
+        res_bf = [tile("res_bf%d" % ph, [P, PACK * HALF], BF16) for ph in range(2)]
+        res_codes = tile("res_codes", [P, N], U32)
+        res_scales = tile("res_scales", [P, N], U8)
 
-        def product(g, out, lhs_codes, lhs_scales, rhs_codes, rhs_scales):
-            r = rows_of(g)
-            nc.tensor.matmul_mx(
-                out=out,
-                lhsT=lhs_codes[r, :].bitcast(FP8X4),
-                lhsT_scale=lhs_scales[r, :],
-                rhs=rhs_codes[r, :].bitcast(FP8X4),
-                rhs_scale=rhs_scales[r, :],
-                start=True,
-                stop=True,
+        def quantize(codes, scales, bf):
+            nc.vector.quantize_mx(out=codes.bitcast(FP8X4), scales=scales, in_=bf[:])
+
+        def make_h(ph, g, on_scalar):
+            h_nodes = tile("h_nodes%d_%d" % (ph, g), [P, HALF], BF16)
+            z = banks[ph][g][:, first]
+            if on_scalar:
+                nc.scalar.activation(out=h_nodes[:], in_=z, func=ACT.Copy, scale=ni_of(g))
+            else:
+                nc.vector.tensor_scalar(out=h_nodes[:], in0=z, scalar1=ni_of(g), scalar2=None, op0=ALU.mult)
+            nc.sync.dma_start(out=h_rows[ph][rows_of(g), :, :], in_=h_nodes[:])
+
+        def fetch_own(ph, g, on_scalar):
+            if on_scalar:
+                nc.scalar.copy(out=own[g][:, half_cols(ph)], in_=banks[ph][g][:, second])
+            else:
+                nc.vector.tensor_copy(out=own[g][:, half_cols(ph)], in_=banks[ph][g][:, second])
+
+        def combine(ph, g):
+            cols = half_cols(ph)
+            nc.vector.scalar_tensor_tensor(
+                out=pre[g][:, cols], in0=banks[ph][g][:, first], scalar=nj_of(g), in1=own[g][:, cols],
+                op0=ALU.mult, op1=ALU.add,
             )
 
-        def features_times_weights(k, banks):
-            for c in range(N // MM_N):
-                h, first = divmod(c * MM_N, HALF)
-                for g in range(G):
-                    piece = weight_piece(k, h, g)
-                    product(
-                        g,
-                        banks[g][:, c * MM_N : (c + 1) * MM_N],
-                        x_codes,
-                        x_scales,
-                        piece[:, first : first + MM_N],
-                        piece[:, HALF:].bitcast(U8)[:, first : first + MM_N],
-                    )
-
-        features_times_weights(0, bank_a)
-        features_times_weights(1, bank_b)
-
-        h_rows = [tile("h_rows%d" % h, [P, PACK, HALF], BF16) for h in range(2)]
-        for h in range(2):
-            cols = slice(HALF * h, HALF * (h + 1))
-            for g in (0, 2, 1, 3):
-                h_nodes = tile("h_nodes%d_%d" % (g, h), [P, HALF], BF16)
-                if g < 2:
-                    nc.scalar.activation(out=h_nodes[:], in_=bank_a[g][:, cols], func=ACT.Copy, scale=ni_col[:, g : g + 1])
-                else:
-                    nc.vector.tensor_scalar(
-                        out=h_nodes[:], in0=bank_a[g][:, cols], scalar1=ni_col[:, g : g + 1], scalar2=None, op0=ALU.mult
-                    )
-                nc.sync.dma_start(out=h_rows[h][rows_of(g), :, :], in_=h_nodes[:])
-
-        own = [tile("own%d" % g, [P, N], F32) for g in range(G)]
-        for g in (0, 2, 1, 3):
-            if g < 2:
-                nc.scalar.copy(out=own[g][:], in_=bank_b[g][:])
-            else:
-                nc.vector.tensor_copy(out=own[g][:], in_=bank_b[g][:])
-
-        h_codes = tile("h_codes", [P, N], U32)
-        h_scales = tile("h_scales", [P, N], U8)
-        y_banks = (bank_a, bank_b)
-        for h in range(2):
-            cols = slice(HALF * h, HALF * (h + 1))
-            h_bf = tile("h_bf%d" % h, [P, PACK * HALF], BF16)
-            interleave_shared(nc, h_bf, h_rows[h])
-            nc.vector.quantize_mx(out=h_codes[:, cols].bitcast(FP8X4), scales=h_scales[:, cols], in_=h_bf[:])
-            for c in range(HALF // MM_N):
-                first = HALF * h + c * MM_N
-                for g in range(G):
-                    product(
-                        g,
-                        y_banks[h][g][:, c * MM_N : (c + 1) * MM_N],
-                        ad_codes,
-                        ad_scales,
-                        h_codes[:, first : first + MM_N],
-                        h_scales[:, first : first + MM_N],
-                    )
-
-        pre = [tile("pre%d" % g, [P, N], F32) for g in range(G)]
-        res_rows = [tile("res_rows%d" % h, [P, PACK, HALF], BF16) for h in range(2)]
-        for h in range(2):
-            cols = slice(HALF * h, HALF * (h + 1))
-            for g in range(G):
-                nc.vector.scalar_tensor_tensor(
-                    out=pre[g][:, cols],
-                    in0=y_banks[h][g][:, :HALF],
-                    scalar=nj_col[:, g : g + 1],
-                    in1=own[g][:, cols],
-                    op0=ALU.mult,
-                    op1=ALU.add,
-                )
-                res_nodes = tile("res_nodes%d_%d" % (g, h), [P, HALF], BF16)
-                nc.scalar.activation(out=res_nodes[:], in_=pre[g][:, cols], func=ACT.Relu)
-                nc.sync.dma_start(out=res_rows[h][rows_of(g), :, :], in_=res_nodes[:])
-
-        for g in range(G):
-            res = tile("res%d" % g, [P, N], F32)
-            if g < 3:
-                nc.vector.tensor_scalar_max(out=res[:], in0=pre[g][:], scalar1=0.0)
-            else:
-                nc.scalar.activation(out=res[:], in_=pre[g][:], func=ACT.Relu)
-            nc.sync.dma_start(out=out_0[NODES * g : NODES * (g + 1), :], in_=res[:])
+        def hand_on(ph, g):
+            res_nodes = tile("res_nodes%d_%d" % (ph, g), [P, HALF], BF16)
+            nc.scalar.activation(out=res_nodes[:], in_=pre[g][:, half_cols(ph)], func=ACT.Relu)
+            nc.sync.dma_start(out=res_rows[ph][rows_of(g), :, :], in_=res_nodes[:])
 
         words = out_1[0].rearrange("p n u -> p (n u)").bitcast(I32)
         scale_rows = out_2[0].bitcast(I32)
-        res_codes = tile("res_codes", [P, N], U32)
-        res_scales = tile("res_scales", [P, N], U8)
+        scale_words = res_scales[:].bitcast(I32)
+
+        interleave_shared(nc, w_bf, w_raw)
+        quantize(home[:, :HALF], home[:, HALF:].bitcast(U8), w_bf)
+        spread(0, nc.sync, nc.scalar)
+        spread(1, nc.sync, nc.sync)
+        out, in_ = interleave_views(x_bf, x_raw, 0, NODES)
+        nc.vector.tensor_copy(out=out, in_=in_)
+        nc.vector.transpose(out=factors[:], in_=factor_rows[:])
+        quantize(x_mx[0][:], x_mx[1][:], x_bf)
+        out, in_ = interleave_views(ad_bf, ad_raw, 0, NODES)
+        nc.vector.tensor_copy(out=out, in_=in_)
+        quantize(ad_mx[0][:], ad_mx[1][:], ad_bf)
+        weight_products(0, 0, (0,))
+        weight_products(0, 1, (1,))
+        make_h(0, 0, True)
+        make_h(1, 1, True)
+        weight_products(0, 0, (1, 2))
+        weight_products(0, 0, (3,))
+        weight_products(0, 1, (2, 3))
+        weight_products(0, 1, (0,))
+        make_h(0, 1, True)
+        make_h(0, 2, False)
+        make_h(0, 3, True)
+        make_h(1, 2, False)
+        make_h(1, 3, True)
+        make_h(1, 0, False)
         for h in range(2):
-            cols = slice(HALF * h, HALF * (h + 1))
-            res_bf = tile("res_bf%d" % h, [P, PACK * HALF], BF16)
-            interleave_shared(nc, res_bf, res_rows[h])
-            nc.vector.quantize_mx(out=res_codes[:, cols].bitcast(FP8X4), scales=res_scales[:, cols], in_=res_bf[:])
+            weight_products(1, h, (0, 2))
+            weight_products(1, h, (1, 3))
+        for h in range(2):
+            for g in (0, 2, 1, 3):
+                fetch_own(h, g, g < 2)
+        for h in range(2):
+            interleave_shared(nc, h_bf[h], h_rows[h])
+            quantize(h_codes[h][:], h_scales[h][:], h_bf[h])
+            edge_products(h, (0, 2))
+            edge_products(h, (1, 3))
+        for h in range(2):
+            for g in (0, 2, 1, 3):
+                combine(h, g)
+                hand_on(h, g)
+
+        for g in range(G):
+            dst = res[g // 2][:, g % 2, :]
+            if g < 3:
+                nc.vector.tensor_scalar_max(out=dst, in0=pre[g][:], scalar1=0.0)
+            else:
+                nc.scalar.activation(out=dst, in_=pre[g][:], func=ACT.Relu)
+            if g % 2 == 1:
+                rows = out_0[NODES * (g - 1) : NODES * (g + 1), :]
+                nc.sync.dma_start(out=rows.rearrange("(g j) n -> j g n", g=2), in_=res[g // 2][:])
+
+        for ph in range(2):
+            cols = half_cols(ph)
+            interleave_shared(nc, res_bf[ph], res_rows[ph])
+            quantize(res_codes[:, cols], res_scales[:, cols], res_bf[ph])
             nc.sync.dma_start(out=words[:, cols], in_=res_codes[:, cols].bitcast(I32))
         for q in range(G):
             engine = nc.scalar if q < 2 else nc.sync
-            engine.dma_start(
-                out=scale_rows[4 * q : 4 * q + 4, :], in_=res_scales[ROWS * q : ROWS * q + 4, :].bitcast(I32)
-            )
+            engine.dma_start(out=scale_rows[4 * q : 4 * q + 4, :], in_=scale_words[ROWS * q : ROWS * q + 4, :])

@@ -20,6 +20,9 @@ ROWS = 32
 HALF = N // 2
 MM_N = 128
 SCALE_WORDS = HALF // 4
+RUN = 4
+FACTOR_STEP = 8
+NJ_ROW = FACTOR_STEP // 2
 VECTOR_COLS = 176
 
 
@@ -27,22 +30,27 @@ def rows_of(g):
     return slice(ROWS * g, ROWS * (g + 1))
 
 
+def half_cols(h):
+    return slice(HALF * h, HALF * (h + 1))
+
+
 def interleave_views(dst, src, lo, hi):
-    out = dst[:, PACK * lo : PACK * hi].rearrange("p (c i t) -> p c t i", i=4, t=PACK)
-    in_ = src[:, :, lo:hi].rearrange("p t (c i) -> p c t i", i=4)
-    return out, in_
+    out = dst[:, PACK * lo : PACK * hi].rearrange("p (c i t) -> p c t i", i=RUN, t=PACK)
+    return out, src[:, :, lo:hi].rearrange("p t (c i) -> p c t i", i=RUN)
 
 
-def interleave_shared(nc, dst, src, vector_cols=VECTOR_COLS):
-    if vector_cols:
-        out, in_ = interleave_views(dst, src, 0, vector_cols)
-        nc.vector.tensor_copy(out=out, in_=in_)
-    out, in_ = interleave_views(dst, src, vector_cols, HALF)
+def interleave_shared(nc, dst, src):
+    out, in_ = interleave_views(dst, src, 0, VECTOR_COLS)
+    nc.vector.tensor_copy(out=out, in_=in_)
+    out, in_ = interleave_views(dst, src, VECTOR_COLS, HALF)
     nc.scalar.copy(out=out, in_=in_)
 
 
-def half_cols(h):
-    return slice(HALF * h, HALF * (h + 1))
+def interleave_shared_relu(nc, dst, src):
+    out, in_ = interleave_views(dst, src, 0, VECTOR_COLS)
+    nc.vector.tensor_scalar_max(out=out, in0=in_, scalar1=0.0)
+    out, in_ = interleave_views(dst, src, VECTOR_COLS, HALF)
+    nc.scalar.activation(out=out, in_=in_, func=ACT.Relu)
 
 
 def tile_rows_pl_gnn_sage_kernel(tc, x, w, ni, ad, wo, nj, out_0, out_1, out_2):
@@ -55,51 +63,51 @@ def tile_rows_pl_gnn_sage_kernel(tc, x, w, ni, ad, wo, nj, out_0, out_1, out_2):
         def tile(name, shape, dtype):
             return sb.tile(shape, dtype, name=name, align_bytes=64)
 
-        banks = [[ps.tile([P, N], F32, name="bank%d_%d" % (ph, g)) for g in range(G)] for ph in range(2)]
-        first, second = slice(0, HALF), slice(HALF, N)
+        def quantize(codes, scales, values):
+            nc.vector.quantize_mx(out=codes.bitcast(FP8X4), scales=scales, in_=values[:])
 
-        w_raw = tile("w_raw", [P, PACK, HALF], F32)
+        banks = [[ps.tile([P, N], F32, name="bank%d_%d" % (h, g)) for g in range(G)] for h in range(2)]
+        front, back = half_cols(0), half_cols(1)
+
+        weights_raw = tile("weights_raw", [P, PACK, HALF], F32)
         x_raw = tile("x_raw", [P, PACK, NODES], F32)
         ad_raw = tile("ad_raw", [P, PACK, NODES], F32)
         factor_rows = tile("factor_rows", [P, ROWS], F32)
-        factors = tile("factors", [P, ROWS], F32)
         home = tile("home", [P, HALF + SCALE_WORDS], U32)
         across = tile("across", [P, HALF + SCALE_WORDS], U32)
         near = [tile("near%d" % k, [P, HALF + SCALE_WORDS], U32) for k in range(2)]
         nc.vector.memset(factor_rows[:], 0.0)
         nc.vector.memset(home[:, HALF:], 0)
-
-        def load_factor(src, row):
-            nc.scalar.dma_start(out=factor_rows[row:P:8, :], in_=src.rearrange("g (q b) o -> q g (b o)", b=ROWS))
-
         for h in range(2):
-            nc.sync.dma_start(out=w_raw[rows_of(h), :, :], in_=w[:, half_cols(h)].rearrange("(p j) n -> p j n", j=PACK))
-            nc.scalar.dma_start(out=w_raw[rows_of(2 + h), :, :], in_=wo[:, half_cols(h)].rearrange("(p j) n -> p j n", j=PACK))
-        nc.sync.dma_start(out=x_raw[:], in_=x.rearrange("g (p j) i -> (g p) j i", j=PACK))
-        nc.sync.dma_start(out=ad_raw[:], in_=ad.rearrange("g (p j) i -> (g p) j i", j=PACK))
-        load_factor(ni, 0)
-        load_factor(nj, 4)
+            for k, (engine, src) in enumerate(((nc.sync, w), (nc.scalar, wo))):
+                engine.dma_start(
+                    out=weights_raw[rows_of(2 * k + h), :, :],
+                    in_=src[:, half_cols(h)].rearrange("(p t) n -> p t n", t=PACK),
+                )
+        nc.sync.dma_start(out=x_raw[:], in_=x.rearrange("g (p t) i -> (g p) t i", t=PACK))
+        nc.sync.dma_start(out=ad_raw[:], in_=ad.rearrange("g (p t) j -> (g p) t j", t=PACK))
+        for row, src in ((0, ni), (NJ_ROW, nj)):
+            nc.scalar.dma_start(
+                out=factor_rows[row:P:FACTOR_STEP, :], in_=src.rearrange("g (q b) o -> q g (b o)", b=ROWS)
+            )
         warm = tile("warm", [P, 1], F32)
         nc.scalar.activation(out=warm[:], in_=home[:, HALF : HALF + 1], func=ACT.Relu)
 
-        def ni_of(g):
-            return factors[:, 8 * g : 8 * g + 1]
+        weights_bf = tile("weights_bf", [P, PACK * HALF], BF16)
+        interleave_shared(nc, weights_bf, weights_raw)
+        quantize(home[:, :HALF], home[:, HALF:].bitcast(U8), weights_bf)
 
-        def nj_of(g):
-            return factors[:, 8 * g + 4 : 8 * g + 5]
-
-        def move(engine, dst, dst_row, src_row, count):
+        def move(engine, dst, dst_quadrant, src_quadrant, quadrants):
             engine.dma_start(
-                out=dst[dst_row : dst_row + count, :].bitcast(I32),
-                in_=home[src_row : src_row + count, :].bitcast(I32),
+                out=dst[ROWS * dst_quadrant : ROWS * (dst_quadrant + quadrants), :].bitcast(I32),
+                in_=home[ROWS * src_quadrant : ROWS * (src_quadrant + quadrants), :].bitcast(I32),
             )
 
         def spread(k, one, other):
-            base = 64 * k
-            move(one, near[k], 32, base, 64)
-            move(other, across, 64 - base, base, 64)
-            move(other, near[k], 96, base, 32)
-            move(one, near[k], 0, base + 32, 32)
+            move(one, near[k], 1, 2 * k, 2)
+            move(other, across, 2 - 2 * k, 2 * k, 2)
+            move(other, near[k], 3, 2 * k, 1)
+            move(one, near[k], 0, 2 * k + 1, 1)
 
         def weight_piece(k, h, g):
             quadrant = 2 * k + h
@@ -109,14 +117,35 @@ def tile_rows_pl_gnn_sage_kernel(tc, x, w, ni, ad, wo, nj, out_0, out_1, out_2):
                 return across
             return near[k]
 
-        def products(lhs, rhs_of, ph, cols, graphs):
-            lhs_codes, lhs_scales = lhs
+        spread(0, nc.sync, nc.scalar)
+        spread(1, nc.sync, nc.sync)
+
+        x_bf = tile("x_bf", [P, PACK * NODES], BF16)
+        ad_bf = tile("ad_bf", [P, PACK * NODES], BF16)
+        x_codes, x_scales = tile("x_codes", [P, NODES], U32), tile("x_scales", [P, NODES], U8)
+        ad_codes, ad_scales = tile("ad_codes", [P, NODES], U32), tile("ad_scales", [P, NODES], U8)
+        factors = tile("factors", [P, ROWS], F32)
+        out, in_ = interleave_views(x_bf, x_raw, 0, NODES)
+        nc.vector.tensor_copy(out=out, in_=in_)
+        nc.vector.transpose(out=factors[:], in_=factor_rows[:])
+        quantize(x_codes[:], x_scales[:], x_bf)
+        out, in_ = interleave_views(ad_bf, ad_raw, 0, NODES)
+        nc.vector.tensor_copy(out=out, in_=in_)
+        quantize(ad_codes[:], ad_scales[:], ad_bf)
+
+        def ni_of(g):
+            return factors[:, FACTOR_STEP * g : FACTOR_STEP * g + 1]
+
+        def nj_of(g):
+            return factors[:, FACTOR_STEP * g + NJ_ROW : FACTOR_STEP * g + NJ_ROW + 1]
+
+        def products(lhs_codes, lhs_scales, rhs_of, h, bank_cols, graphs):
             for c in range(0, HALF, MM_N):
                 for g in graphs:
                     r = rows_of(g)
                     rhs_codes, rhs_scales = rhs_of(g)
                     nc.tensor.matmul_mx(
-                        out=banks[ph][g][:, cols.start + c : cols.start + c + MM_N],
+                        out=banks[h][g][:, bank_cols.start + c : bank_cols.start + c + MM_N],
                         lhsT=lhs_codes[r, :].bitcast(FP8X4),
                         lhsT_scale=lhs_scales[r, :],
                         rhs=rhs_codes[r, c : c + MM_N].bitcast(FP8X4),
@@ -130,118 +159,110 @@ def tile_rows_pl_gnn_sage_kernel(tc, x, w, ni, ad, wo, nj, out_0, out_1, out_2):
                 piece = weight_piece(k, h, g)
                 return piece[:, :HALF], piece[:, HALF:].bitcast(U8)
 
-            products(x_mx, rhs_of, h, (first, second)[k], graphs)
+            products(x_codes, x_scales, rhs_of, h, (front, back)[k], graphs)
 
-        def edge_products(h, graphs):
-            products(ad_mx, lambda g: (h_codes[h], h_scales[h]), h, first, graphs)
+        h_rows = [tile("h_rows%d" % h, [P, PACK, HALF], BF16) for h in range(2)]
 
-        w_bf = tile("w_bf", [P, PACK * HALF], BF16)
-        x_bf = tile("x_bf", [P, PACK * NODES], BF16)
-        ad_bf = tile("ad_bf", [P, PACK * NODES], BF16)
-        x_mx = (tile("x_codes", [P, NODES], U32), tile("x_scales", [P, NODES], U8))
-        ad_mx = (tile("ad_codes", [P, NODES], U32), tile("ad_scales", [P, NODES], U8))
-        h_rows = [tile("h_rows%d" % ph, [P, PACK, HALF], BF16) for ph in range(2)]
-        h_bf = [tile("h_bf%d" % ph, [P, PACK * HALF], BF16) for ph in range(2)]
-        h_codes = [tile("h_codes%d" % ph, [P, HALF], U32) for ph in range(2)]
-        h_scales = [tile("h_scales%d" % ph, [P, HALF], U8) for ph in range(2)]
-        own = [tile("own%d" % g, [P, N], F32) for g in range(G)]
-        pre = [tile("pre%d" % g, [P, N], F32) for g in range(G)]
-        res = [tile("res%d" % k, [P, 2, N], F32) for k in range(2)]
-        res_rows = [tile("res_rows%d" % ph, [P, PACK, HALF], BF16) for ph in range(2)]
-        res_bf = [tile("res_bf%d" % ph, [P, PACK * HALF], BF16) for ph in range(2)]
-        res_codes = tile("res_codes", [P, N], U32)
-        res_scales = tile("res_scales", [P, N], U8)
-
-        def quantize(codes, scales, bf):
-            nc.vector.quantize_mx(out=codes.bitcast(FP8X4), scales=scales, in_=bf[:])
-
-        def make_h(ph, g, on_scalar):
-            h_nodes = tile("h_nodes%d_%d" % (ph, g), [P, HALF], BF16)
-            z = banks[ph][g][:, first]
+        def make_h(h, g, on_scalar):
+            h_nodes = tile("h_nodes%d_%d" % (h, g), [P, HALF], BF16)
+            z = banks[h][g][:, front]
             if on_scalar:
                 nc.scalar.activation(out=h_nodes[:], in_=z, func=ACT.Copy, scale=ni_of(g))
             else:
                 nc.vector.tensor_scalar(out=h_nodes[:], in0=z, scalar1=ni_of(g), scalar2=None, op0=ALU.mult)
-            nc.sync.dma_start(out=h_rows[ph][rows_of(g), :, :], in_=h_nodes[:])
+            nc.sync.dma_start(out=h_rows[h][rows_of(g), :, :], in_=h_nodes[:])
 
-        def fetch_own(ph, g, on_scalar):
-            if on_scalar:
-                nc.scalar.copy(out=own[g][:, half_cols(ph)], in_=banks[ph][g][:, second])
-            else:
-                nc.vector.tensor_copy(out=own[g][:, half_cols(ph)], in_=banks[ph][g][:, second])
-
-        def combine(ph, g):
-            cols = half_cols(ph)
-            nc.vector.scalar_tensor_tensor(
-                out=pre[g][:, cols], in0=banks[ph][g][:, first], scalar=nj_of(g), in1=own[g][:, cols],
-                op0=ALU.mult, op1=ALU.add,
-            )
-
-        def hand_on(ph, g):
-            res_nodes = tile("res_nodes%d_%d" % (ph, g), [P, HALF], BF16)
-            nc.scalar.activation(out=res_nodes[:], in_=pre[g][:, half_cols(ph)], func=ACT.Relu)
-            nc.sync.dma_start(out=res_rows[ph][rows_of(g), :, :], in_=res_nodes[:])
-
-        words = out_1[0].rearrange("p n u -> p (n u)").bitcast(I32)
-        scale_rows = out_2[0].bitcast(I32)
-        scale_words = res_scales[:].bitcast(I32)
-
-        interleave_shared(nc, w_bf, w_raw)
-        quantize(home[:, :HALF], home[:, HALF:].bitcast(U8), w_bf)
-        spread(0, nc.sync, nc.scalar)
-        spread(1, nc.sync, nc.sync)
-        out, in_ = interleave_views(x_bf, x_raw, 0, NODES)
-        nc.vector.tensor_copy(out=out, in_=in_)
-        nc.vector.transpose(out=factors[:], in_=factor_rows[:])
-        quantize(x_mx[0][:], x_mx[1][:], x_bf)
-        out, in_ = interleave_views(ad_bf, ad_raw, 0, NODES)
-        nc.vector.tensor_copy(out=out, in_=in_)
-        quantize(ad_mx[0][:], ad_mx[1][:], ad_bf)
-        weight_products(0, 0, (0,))
-        weight_products(0, 1, (1,))
-        make_h(0, 0, True)
-        make_h(1, 1, True)
+        for h in range(2):
+            weight_products(0, h, (h,))
+        for h in range(2):
+            make_h(h, h, on_scalar=True)
         weight_products(0, 0, (1, 2))
         weight_products(0, 0, (3,))
         weight_products(0, 1, (2, 3))
         weight_products(0, 1, (0,))
-        make_h(0, 1, True)
-        make_h(0, 2, False)
-        make_h(0, 3, True)
-        make_h(1, 2, False)
-        make_h(1, 3, True)
-        make_h(1, 0, False)
-        for h in range(2):
-            weight_products(1, h, (0, 2))
-            weight_products(1, h, (1, 3))
-        for h in range(2):
-            for g in (0, 2, 1, 3):
-                fetch_own(h, g, g < 2)
-        for h in range(2):
-            interleave_shared(nc, h_bf[h], h_rows[h])
-            quantize(h_codes[h][:], h_scales[h][:], h_bf[h])
-            edge_products(h, (0, 2))
-            edge_products(h, (1, 3))
-        for h in range(2):
-            for g in (0, 2, 1, 3):
-                combine(h, g)
-                hand_on(h, g)
+        for turn, (h, g) in enumerate(((0, 1), (0, 2), (0, 3), (1, 2), (1, 3), (1, 0))):
+            make_h(h, g, on_scalar=(turn % 2 == 0))
 
-        for g in range(G):
-            dst = res[g // 2][:, g % 2, :]
-            if g < 3:
-                nc.vector.tensor_scalar_max(out=dst, in0=pre[g][:], scalar1=0.0)
+        own = [tile("own%d" % g, [P, N], F32) for g in range(G)]
+        pairs = ((0, 2), (1, 3))
+        for h in range(2):
+            for pair in pairs:
+                weight_products(1, h, pair)
+        for h in range(2):
+            for scalar_g, vector_g in pairs:
+                nc.scalar.copy(out=own[scalar_g][:, half_cols(h)], in_=banks[h][scalar_g][:, back])
+                nc.vector.tensor_copy(out=own[vector_g][:, half_cols(h)], in_=banks[h][vector_g][:, back])
+
+        for h in range(2):
+            h_bf = tile("h_bf%d" % h, [P, PACK * HALF], BF16)
+            h_codes, h_scales = tile("h_codes%d" % h, [P, HALF], U32), tile("h_scales%d" % h, [P, HALF], U8)
+            interleave_shared(nc, h_bf, h_rows[h])
+            quantize(h_codes[:], h_scales[:], h_bf)
+            for pair in pairs:
+                products(ad_codes, ad_scales, lambda g: (h_codes, h_scales), h, front, pair)
+
+        pre = [tile("pre%d" % g, [P, N], F32) for g in range(G)]
+        res_rows = [tile("res_rows%d" % h, [P, PACK, HALF], BF16) for h in range(2)]
+
+        def combine(out, h, g):
+            nc.vector.scalar_tensor_tensor(
+                out=out,
+                in0=banks[h][g][:, front],
+                scalar=nj_of(g),
+                in1=own[g][:, half_cols(h)],
+                op0=ALU.mult,
+                op1=ALU.add,
+            )
+
+        def combine_and_send(h, g):
+            res_nodes = tile("res_nodes%d_%d" % (h, g), [P, HALF], BF16)
+            combine(pre[g][:, half_cols(h)], h, g)
+            nc.scalar.activation(out=res_nodes[:], in_=pre[g][:, half_cols(h)], func=ACT.Relu)
+            nc.sync.dma_start(out=res_rows[h][rows_of(g), :, :], in_=res_nodes[:])
+
+        def send_rounded_sum(h, g):
+            res_nodes = tile("res_nodes%d_%d" % (h, g), [P, HALF], BF16)
+            combine(res_nodes[:], h, g)
+            nc.scalar.dma_start(out=res_rows[h][rows_of(g), :, :], in_=res_nodes[:])
+
+        def store_result(g, on_scalar):
+            res = tile("res%d" % g, [P, N], F32)
+            if on_scalar:
+                nc.scalar.activation(out=res[:], in_=pre[g][:], func=ACT.Relu)
             else:
-                nc.scalar.activation(out=dst, in_=pre[g][:], func=ACT.Relu)
-            if g % 2 == 1:
-                rows = out_0[NODES * (g - 1) : NODES * (g + 1), :]
-                nc.sync.dma_start(out=rows.rearrange("(g j) n -> j g n", g=2), in_=res[g // 2][:])
+                nc.vector.tensor_scalar_max(out=res[:], in0=pre[g][:], scalar1=0.0)
+            nc.sync.dma_start(out=out_0[NODES * g : NODES * (g + 1), :], in_=res[:])
 
-        for ph in range(2):
-            cols = half_cols(ph)
-            interleave_shared(nc, res_bf[ph], res_rows[ph])
-            quantize(res_codes[:, cols], res_scales[:, cols], res_bf[ph])
+        early_graphs, last_graphs = (0, 1), (2, 3)
+        for pair in pairs:
+            for g in pair:
+                combine_and_send(0, g)
+        for g in early_graphs:
+            combine_and_send(1, g)
+        for g in last_graphs:
+            send_rounded_sum(1, g)
+        for g in early_graphs:
+            store_result(g, on_scalar=(g == early_graphs[-1]))
+        for g in last_graphs:
+            combine(pre[g][:, half_cols(1)], 1, g)
+        for g in last_graphs:
+            store_result(g, on_scalar=False)
+
+        words = out_1[0].rearrange("p n t -> p (n t)").bitcast(I32)
+        scale_rows = out_2[0].bitcast(I32)
+        res_bf = [tile("res_bf%d" % h, [P, PACK * HALF], BF16) for h in range(2)]
+        res_codes = tile("res_codes", [P, N], U32)
+        res_scales = tile("res_scales", [P, N], U8)
+        interleave_shared(nc, res_bf[0], res_rows[0])
+        interleave_shared_relu(nc, res_bf[1], res_rows[1])
+        for h in range(2):
+            cols = half_cols(h)
+            quantize(res_codes[:, cols], res_scales[:, cols], res_bf[h])
             nc.sync.dma_start(out=words[:, cols], in_=res_codes[:, cols].bitcast(I32))
-        for q in range(G):
-            engine = nc.scalar if q < 2 else nc.sync
-            engine.dma_start(out=scale_rows[4 * q : 4 * q + 4, :], in_=scale_words[ROWS * q : ROWS * q + 4, :])
+        blocks = NODES // 32
+        for g in range(G):
+            engine = nc.scalar if g < 2 else nc.sync
+            engine.dma_start(
+                out=scale_rows[blocks * g : blocks * (g + 1), :],
+                in_=res_scales[ROWS * g : ROWS * g + blocks, :].bitcast(I32),
+            )

from contextlib import ExitStack

import concourse.mybir as mybir

G, D, NODES, N = 4, 128, 128, 512
FLOPS = 3 * 2 * G * D * NODES * N

F32 = mybir.dt.float32
BF16 = mybir.dt.bfloat16
I32 = mybir.dt.int32
U32 = mybir.dt.uint32
U8 = mybir.dt.uint8
FP8X4 = mybir.dt.float8_e4m3fn_x4
ACT = mybir.ActivationFunctionType
ALU = mybir.AluOpType

P = 128
PACK = 4
ROWS = 32
HALF = N // 2
MM_N = 128
SCALE_WORDS = HALF // 4
RUN = 4
FACTOR_STEP = 8
NJ_ROW = FACTOR_STEP // 2
VECTOR_COLS = 176


def rows_of(g):
    return slice(ROWS * g, ROWS * (g + 1))


def half_cols(h):
    return slice(HALF * h, HALF * (h + 1))


def interleave_views(dst, src, lo, hi):
    out = dst[:, PACK * lo : PACK * hi].rearrange("p (c i t) -> p c t i", i=RUN, t=PACK)
    return out, src[:, :, lo:hi].rearrange("p t (c i) -> p c t i", i=RUN)


def interleave_shared(nc, dst, src):
    out, in_ = interleave_views(dst, src, 0, VECTOR_COLS)
    nc.vector.tensor_copy(out=out, in_=in_)
    out, in_ = interleave_views(dst, src, VECTOR_COLS, HALF)
    nc.scalar.copy(out=out, in_=in_)


def interleave_shared_relu(nc, dst, src):
    out, in_ = interleave_views(dst, src, 0, VECTOR_COLS)
    nc.vector.tensor_scalar_max(out=out, in0=in_, scalar1=0.0)
    out, in_ = interleave_views(dst, src, VECTOR_COLS, HALF)
    nc.scalar.activation(out=out, in_=in_, func=ACT.Relu)


def tile_rows_pl_gnn_sage_kernel(tc, x, w, ni, ad, wo, nj, out_0, out_1, out_2):
    nc = tc.nc
    with ExitStack() as ctx:
        sb = ctx.enter_context(tc.tile_pool(name="sb", bufs=1))
        ps = ctx.enter_context(tc.psum_pool(name="ps", bufs=1))
        ctx.enter_context(tc.manual_schedule())

        def tile(name, shape, dtype):
            return sb.tile(shape, dtype, name=name, align_bytes=64)

        def quantize(codes, scales, values):
            nc.vector.quantize_mx(out=codes.bitcast(FP8X4), scales=scales, in_=values[:])

        banks = [[ps.tile([P, N], F32, name="bank%d_%d" % (h, g)) for g in range(G)] for h in range(2)]
        front, back = half_cols(0), half_cols(1)

        weights_raw = tile("weights_raw", [P, PACK, HALF], F32)
        x_raw = tile("x_raw", [P, PACK, NODES], F32)
        ad_raw = tile("ad_raw", [P, PACK, NODES], F32)
        factor_rows = tile("factor_rows", [P, ROWS], F32)
        home = tile("home", [P, HALF + SCALE_WORDS], U32)
        across = tile("across", [P, HALF + SCALE_WORDS], U32)
        near = [tile("near%d" % k, [P, HALF + SCALE_WORDS], U32) for k in range(2)]
        nc.vector.memset(factor_rows[:], 0.0)
        nc.vector.memset(home[:, HALF:], 0)
        for h in range(2):
            for k, (engine, src) in enumerate(((nc.sync, w), (nc.scalar, wo))):
                engine.dma_start(
                    out=weights_raw[rows_of(2 * k + h), :, :],
                    in_=src[:, half_cols(h)].rearrange("(p t) n -> p t n", t=PACK),
                )
        nc.sync.dma_start(out=x_raw[:], in_=x.rearrange("g (p t) i -> (g p) t i", t=PACK))
        nc.sync.dma_start(out=ad_raw[:], in_=ad.rearrange("g (p t) j -> (g p) t j", t=PACK))
        for row, src in ((0, ni), (NJ_ROW, nj)):
            nc.scalar.dma_start(
                out=factor_rows[row:P:FACTOR_STEP, :], in_=src.rearrange("g (q b) o -> q g (b o)", b=ROWS)
            )
        warm = tile("warm", [P, 1], F32)
        nc.scalar.activation(out=warm[:], in_=home[:, HALF : HALF + 1], func=ACT.Relu)

        weights_bf = tile("weights_bf", [P, PACK * HALF], BF16)
        interleave_shared(nc, weights_bf, weights_raw)
        quantize(home[:, :HALF], home[:, HALF:].bitcast(U8), weights_bf)

        def move(engine, dst, dst_quadrant, src_quadrant, quadrants):
            engine.dma_start(
                out=dst[ROWS * dst_quadrant : ROWS * (dst_quadrant + quadrants), :].bitcast(I32),
                in_=home[ROWS * src_quadrant : ROWS * (src_quadrant + quadrants), :].bitcast(I32),
            )

        def spread(k, one, other):
            move(one, near[k], 1, 2 * k, 2)
            move(other, across, 2 - 2 * k, 2 * k, 2)
            move(other, near[k], 3, 2 * k, 1)
            move(one, near[k], 0, 2 * k + 1, 1)

        def weight_piece(k, h, g):
            quadrant = 2 * k + h
            if g == quadrant:
                return home
            if g == (quadrant + 2) % G:
                return across
            return near[k]

        spread(0, nc.sync, nc.scalar)
        spread(1, nc.sync, nc.sync)

        x_bf = tile("x_bf", [P, PACK * NODES], BF16)
        ad_bf = tile("ad_bf", [P, PACK * NODES], BF16)
        x_codes, x_scales = tile("x_codes", [P, NODES], U32), tile("x_scales", [P, NODES], U8)
        ad_codes, ad_scales = tile("ad_codes", [P, NODES], U32), tile("ad_scales", [P, NODES], U8)
        factors = tile("factors", [P, ROWS], F32)
        out, in_ = interleave_views(x_bf, x_raw, 0, NODES)
        nc.vector.tensor_copy(out=out, in_=in_)
        nc.vector.transpose(out=factors[:], in_=factor_rows[:])
        quantize(x_codes[:], x_scales[:], x_bf)
        out, in_ = interleave_views(ad_bf, ad_raw, 0, NODES)
        nc.vector.tensor_copy(out=out, in_=in_)
        quantize(ad_codes[:], ad_scales[:], ad_bf)

        def ni_of(g):
            return factors[:, FACTOR_STEP * g : FACTOR_STEP * g + 1]

        def nj_of(g):
            return factors[:, FACTOR_STEP * g + NJ_ROW : FACTOR_STEP * g + NJ_ROW + 1]

        def products(lhs_codes, lhs_scales, rhs_of, h, bank_cols, graphs):
            for c in range(0, HALF, MM_N):
                for g in graphs:
                    r = rows_of(g)
                    rhs_codes, rhs_scales = rhs_of(g)
                    nc.tensor.matmul_mx(
                        out=banks[h][g][:, bank_cols.start + c : bank_cols.start + c + MM_N],
                        lhsT=lhs_codes[r, :].bitcast(FP8X4),
                        lhsT_scale=lhs_scales[r, :],
                        rhs=rhs_codes[r, c : c + MM_N].bitcast(FP8X4),
                        rhs_scale=rhs_scales[r, c : c + MM_N],
                        start=True,
                        stop=True,
                    )

        def weight_products(k, h, graphs):
            def rhs_of(g):
                piece = weight_piece(k, h, g)
                return piece[:, :HALF], piece[:, HALF:].bitcast(U8)

            products(x_codes, x_scales, rhs_of, h, (front, back)[k], graphs)

        h_rows = [tile("h_rows%d" % h, [P, PACK, HALF], BF16) for h in range(2)]

        def make_h(h, g, on_scalar):
            h_nodes = tile("h_nodes%d_%d" % (h, g), [P, HALF], BF16)
            z = banks[h][g][:, front]
            if on_scalar:
                nc.scalar.activation(out=h_nodes[:], in_=z, func=ACT.Copy, scale=ni_of(g))
            else:
                nc.vector.tensor_scalar(out=h_nodes[:], in0=z, scalar1=ni_of(g), scalar2=None, op0=ALU.mult)
            nc.sync.dma_start(out=h_rows[h][rows_of(g), :, :], in_=h_nodes[:])

        for h in range(2):
            weight_products(0, h, (h,))
        for h in range(2):
            make_h(h, h, on_scalar=True)
        weight_products(0, 0, (1, 2))
        weight_products(0, 0, (3,))
        weight_products(0, 1, (2, 3))
        weight_products(0, 1, (0,))
        for turn, (h, g) in enumerate(((0, 1), (0, 2), (0, 3), (1, 2), (1, 3), (1, 0))):
            make_h(h, g, on_scalar=(turn % 2 == 0))

        own = [tile("own%d" % g, [P, N], F32) for g in range(G)]
        pairs = ((0, 2), (1, 3))
        for h in range(2):
            for pair in pairs:
                weight_products(1, h, pair)
        for h in range(2):
            for scalar_g, vector_g in pairs:
                nc.scalar.copy(out=own[scalar_g][:, half_cols(h)], in_=banks[h][scalar_g][:, back])
                nc.vector.tensor_copy(out=own[vector_g][:, half_cols(h)], in_=banks[h][vector_g][:, back])

        for h in range(2):
            h_bf = tile("h_bf%d" % h, [P, PACK * HALF], BF16)
            h_codes, h_scales = tile("h_codes%d" % h, [P, HALF], U32), tile("h_scales%d" % h, [P, HALF], U8)
            interleave_shared(nc, h_bf, h_rows[h])
            quantize(h_codes[:], h_scales[:], h_bf)
            for pair in pairs:
                products(ad_codes, ad_scales, lambda g: (h_codes, h_scales), h, front, pair)

        pre = [tile("pre%d" % g, [P, N], F32) for g in range(G)]
        res_rows = [tile("res_rows%d" % h, [P, PACK, HALF], BF16) for h in range(2)]

        def combine(out, h, g):
            nc.vector.scalar_tensor_tensor(
                out=out,
                in0=banks[h][g][:, front],
                scalar=nj_of(g),
                in1=own[g][:, half_cols(h)],
                op0=ALU.mult,
                op1=ALU.add,
            )

        def combine_and_send(h, g):
            res_nodes = tile("res_nodes%d_%d" % (h, g), [P, HALF], BF16)
            combine(pre[g][:, half_cols(h)], h, g)
            nc.scalar.activation(out=res_nodes[:], in_=pre[g][:, half_cols(h)], func=ACT.Relu)
            nc.sync.dma_start(out=res_rows[h][rows_of(g), :, :], in_=res_nodes[:])

        def send_rounded_sum(h, g):
            res_nodes = tile("res_nodes%d_%d" % (h, g), [P, HALF], BF16)
            combine(res_nodes[:], h, g)
            nc.scalar.dma_start(out=res_rows[h][rows_of(g), :, :], in_=res_nodes[:])

        def store_result(g, on_scalar):
            res = tile("res%d" % g, [P, N], F32)
            if on_scalar:
                nc.scalar.activation(out=res[:], in_=pre[g][:], func=ACT.Relu)
            else:
                nc.vector.tensor_scalar_max(out=res[:], in0=pre[g][:], scalar1=0.0)
            nc.sync.dma_start(out=out_0[NODES * g : NODES * (g + 1), :], in_=res[:])

        early_graphs, last_graphs = (0, 1), (2, 3)
        for pair in pairs:
            for g in pair:
                combine_and_send(0, g)
        for g in early_graphs:
            combine_and_send(1, g)
        for g in last_graphs:
            send_rounded_sum(1, g)
        for g in early_graphs:
            store_result(g, on_scalar=(g == early_graphs[-1]))
        for g in last_graphs:
            combine(pre[g][:, half_cols(1)], 1, g)
        for g in last_graphs:
            store_result(g, on_scalar=False)

        words = out_1[0].rearrange("p n t -> p (n t)").bitcast(I32)
        scale_rows = out_2[0].bitcast(I32)
        res_bf = [tile("res_bf%d" % h, [P, PACK * HALF], BF16) for h in range(2)]
        res_codes = tile("res_codes", [P, N], U32)
        res_scales = tile("res_scales", [P, N], U8)
        interleave_shared(nc, res_bf[0], res_rows[0])
        interleave_shared_relu(nc, res_bf[1], res_rows[1])
        for h in range(2):
            cols = half_cols(h)
            quantize(res_codes[:, cols], res_scales[:, cols], res_bf[h])
            nc.sync.dma_start(out=words[:, cols], in_=res_codes[:, cols].bitcast(I32))
        blocks = NODES // 32
        for g in range(G):
            engine = nc.scalar if g < 2 else nc.sync
            engine.dma_start(
                out=scale_rows[blocks * g : blocks * (g + 1), :],
                in_=res_scales[ROWS * g : ROWS * g + blocks, :].bitcast(I32),
            )
